import numpy as np
import ml_dtypes


def mxq(x, axis, fmt="e4m3"):
    dtype, down = {"e4m3": (ml_dtypes.float8_e4m3fn, 7), "e5m2": (ml_dtypes.float8_e5m2, 14)}[fmt]
    v = np.moveaxis(np.asarray(x, np.float32).astype(ml_dtypes.bfloat16).astype(np.float64), axis, -1)
    blocks = v.reshape(v.shape[:-1] + (-1, 32))
    amax = np.abs(blocks).max(-1, keepdims=True)
    byte = np.maximum(np.where(amax > 0, np.frexp(amax)[1] - 1 + 127, 0) - down, 1)
    scale = np.exp2(byte - 127.0)
    codes = (blocks / scale).astype(np.float32).astype(dtype).astype(np.float64)
    return np.moveaxis((codes * scale).reshape(v.shape), -1, axis)


WIDE = False


def mx_kscale(k):
    if not WIDE:
        return np.ones(k)
    levels = np.array([30, -30])
    if k % 512:
        return np.exp2(np.random.permutation(np.resize(levels, k // 32))).repeat(32)
    a = np.empty((k // 512, 16))
    for p in range(k // 512):
        a[p, :8] = np.random.permutation(np.resize(levels, 8))
        for g in range(8):
            far = levels[np.abs(levels - a[p, g]) >= 10]
            a[p, g + 8] = far[np.random.randint(len(far))]
    return np.exp2(a.ravel()).repeat(32)


def f64(x):
    return np.asarray(x).astype(np.float64)


def striped(idx):
    return np.tile(np.asarray(idx).reshape(-1, 16).T, (8, 1)).astype(np.uint16)


def unstriped(offs):
    return offs[:16].T.reshape(-1).astype(np.int64)


E2M1 = np.array([0.0, 0.5, 1.0, 1.5, 2.0, 3.0, 4.0, 6.0, -0.0, -0.5, -1.0, -1.5, -2.0, -3.0, -4.0, -6.0])


def pack_weight(w, fmt):
    k, n = w.shape
    w = f64(np.asarray(w, np.float32).astype(ml_dtypes.bfloat16)).reshape(k // 32, 32, n)
    amax = np.abs(w).max(1)
    if fmt in ("e4m3", "e5m2"):
        byte = np.frexp(amax)[1] - 1 + 127 - (7 if fmt == "e4m3" else 14)
    else:
        mant, ex = np.frexp(amax / 6.0)
        byte = np.where(mant > 0.5, ex, ex - 1) + 127
    byte = np.clip(np.where(amax > 0, byte, 1), 1, 254)
    scaled = (w * np.exp2(127.0 - byte)[:, None, :]).reshape(k, n).astype(np.float32)
    by_word = np.ascontiguousarray(scaled.reshape(k // 512, 128, 4, n).transpose(0, 1, 3, 2))
    if fmt in ("e4m3", "e5m2"):
        words = by_word.astype(ml_dtypes.float8_e4m3fn if fmt == "e4m3" else ml_dtypes.float8_e5m2).view(np.uint8)
    else:
        c = by_word.astype(ml_dtypes.float4_e2m1fn).view(np.uint8) & 0xF
        words = (c[..., 0::2] | (c[..., 1::2] << 4)).reshape(k // 512, 128, 2 * n)
    return np.ascontiguousarray(words), np.ascontiguousarray(byte.astype(np.uint8).reshape(k // 512, 16, n))


def unpack_weight(words, scales, fmt):
    g, _, n = scales.shape
    words = np.ascontiguousarray(words).reshape(g, 128, n, -1)
    if fmt in ("e4m3", "e5m2"):
        vals = words.view(ml_dtypes.float8_e4m3fn if fmt == "e4m3" else ml_dtypes.float8_e5m2).astype(np.float64)
    else:
        nib = np.empty((g, 128, n, 4), np.uint8)
        nib[..., 0::2] = words & 0xF
        nib[..., 1::2] = words >> 4
        vals = E2M1[nib]
    vals = vals * np.repeat(np.exp2(scales.astype(np.float64) - 127.0), 8, axis=1)[..., None]
    return vals.transpose(0, 1, 3, 2).reshape(g * 512, n)


def sgn(shape):
    return np.random.uniform(0.5, 2.0, shape) * np.where(np.random.standard_normal(shape) < 0, -1.0, 1.0)


K, T, J, R, V, O, N, E = 512, 1024, 256, 512, 1024, 128, 256, 256


def setup_inputs():
    n = np.random.standard_normal
    idx = np.random.permutation(V)[:R]
    idx2 = np.random.permutation(T)[:J]
    idx3 = np.random.permutation(J)[:O]
    idx4 = np.random.permutation(E)[:O]
    idx5 = np.random.permutation(E)[:O]
    fk = mx_kscale(K)
    fr = mx_kscale(R)
    xtp = pack_weight(n((K, T)) / fk[:, None], "e5m2")
    wtp = pack_weight(n((K, V)) * 1 / np.sqrt(K) * fk[:, None], "e2m1")
    wbp = pack_weight(n((R, N)) * 1 / np.sqrt(R) / fr[:, None], "e2m1")
    wcp = pack_weight(n((R, N)) * 1 / np.sqrt(R) / fr[:, None], "e4m3")
    return {
        "xt_words": xtp[0],
        "xt_scales": xtp[1],
        "wt_words": wtp[0],
        "wt_scales": wtp[1],
        "sa": (sgn((R, 1)) * fr[:, None]).astype(np.float32),
        "wb_words": wbp[0],
        "wb_scales": wbp[1],
        "wc_words": wcp[0],
        "wc_scales": wcp[1],
        "so": (np.random.uniform(0.5, 1.6, (N, 1))).astype(np.float32),
        "sp": (np.random.uniform(0.5, 1.6, (N, 1))).astype(np.float32),
        "offs": striped(idx),
        "offs2": striped(idx2),
        "offs3": striped(idx3),
        "offs4": striped(idx4),
        "offs5": striped(idx5),
    }


def reference(xt_words, xt_scales, wt_words, wt_scales, sa, wb_words, wb_scales, wc_words, wc_scales, so, sp, offs, offs2, offs3, offs4, offs5):
    idx = unstriped(offs)
    idx2 = unstriped(offs2)
    idx3 = unstriped(offs3)
    idx4 = unstriped(offs4)
    idx5 = unstriped(offs5)
    xtu = unpack_weight(xt_words, xt_scales, "e5m2")
    wtu = unpack_weight(wt_words, wt_scales, "e2m1")
    wbu = unpack_weight(wb_words, wb_scales, "e2m1")
    wcu = unpack_weight(wc_words, wc_scales, "e4m3")
    wtidxg = wtu[:, idx]
    xtidx2g = xtu[:, idx2]
    a = wtidxg.T @ xtidx2g
    hid = a[:, idx3] * f64(sa)
    hidq = mxq(hid, 0, "e4m3")
    p = wbu.T @ hidq
    q = wcu.T @ hidq
    pa = np.zeros((N, E))
    pa[:, idx4] = p * f64(so)
    pb = np.zeros((N, E))
    pb[:, idx5] = q * f64(sp)
    y = np.maximum(pa, pb)
    return y

@@ -1,0 +1,121 @@
+from contextlib import ExitStack
+
+import concourse.mybir as mybir
+
+F32 = mybir.dt.float32
+BF16 = mybir.dt.bfloat16
+I32 = mybir.dt.int32
+U32 = mybir.dt.uint32
+U16 = mybir.dt.uint16
+U8 = mybir.dt.uint8
+E4M3X4 = mybir.dt.float8_e4m3fn_x4
+E5M2X4 = mybir.dt.float8_e5m2_x4
+E2M1X4 = mybir.dt.float4_e2m1fn_x4
+COPY = mybir.ActivationFunctionType.Copy
+MAX = mybir.AluOpType.max
+
+K, T, J, R, V, O, N, E = 512, 1024, 256, 512, 1024, 128, 256, 256
+P = 128
+PACK = 4
+QUADS = 4
+FLOPS = 2 * K * R * J + 2 * 2 * R * N * O
+
+
+def tile_list_twooutcomes_kernel(tc, xt_words, xt_scales, wt_words, wt_scales, sa, wb_words, wb_scales,
+                                     wc_words, wc_scales, so, sp, offs, offs2, offs3, offs4, offs5, out):
+    nc = tc.nc
+    with ExitStack() as ctx:
+        sb = ctx.enter_context(tc.tile_pool(name="sb", bufs=1))
+        ps = ctx.enter_context(tc.psum_pool(name="ps", bufs=1))
+
+        def load_list(src, name):
+            tile = sb.tile(list(src.shape), U16, name=name)
+            nc.sync.dma_start(tile[:], src)
+            return tile
+
+        def zeroed_plane(width, name):
+            plane = sb.tile([P, width], U8, name=name, align_bytes=64)
+            nc.vector.memset(plane[:].bitcast(I32), 0)
+            return plane
+
+        def load_plane(plane, scales):
+            for q in range(QUADS):
+                nc.sync.dma_start(plane[32 * q : 32 * q + 4, :].bitcast(I32),
+                                  scales[0, 4 * q : 4 * q + 4, :].bitcast(I32))
+
+        wt_plane = zeroed_plane(V, "wt_plane")
+        xt_plane = zeroed_plane(T, "xt_plane")
+        wb_plane = zeroed_plane(N, "wb_plane")
+        wc_plane = zeroed_plane(N, "wc_plane")
+        pages = [[sb.tile([P, E], F32, name="page%d%d" % (s, h)) for h in range(N // P)] for s in range(2)]
+        for h in range(N // P):
+            for s in range(2):
+                nc.vector.memset(pages[s][h][:], 0.0)
+
+        list_r = load_list(offs, "list_r")
+        load_plane(wt_plane, wt_scales)
+        wt_tab = sb.tile([P, V], U16, name="wt_tab", align_bytes=64)
+        nc.sync.dma_start(wt_tab[:].bitcast(I32), wt_words[0].bitcast(I32))
+        list_j = load_list(offs2, "list_j")
+        xt_tab = sb.tile([P, T], I32, name="xt_tab", align_bytes=64)
+        nc.sync.dma_start(xt_tab[:], xt_words[0].rearrange("p n t -> p (n t)").bitcast(I32))
+        load_plane(xt_plane, xt_scales)
+        list_o = load_list(offs3, "list_o")
+        sa_sb = sb.tile([P, PACK], F32, name="sa_sb")
+        nc.sync.dma_start(sa_sb[:], sa.rearrange("(p t) o -> p (t o)", t=PACK))
+        wb_sb = sb.tile([P, N], U16, name="wb_sb", align_bytes=64)
+        nc.sync.dma_start(wb_sb[:].bitcast(I32), wb_words[0].bitcast(I32))
+        wc_sb = sb.tile([P, N], I32, name="wc_sb", align_bytes=64)
+        nc.sync.dma_start(wc_sb[:], wc_words[0].rearrange("p n t -> p (n t)").bitcast(I32))
+        load_plane(wb_plane, wb_scales)
+        load_plane(wc_plane, wc_scales)
+        list_a = load_list(offs4, "list_a")
+        list_b = load_list(offs5, "list_b")
+        so_sb = sb.tile([P, N // P], F32, name="so_sb")
+        sp_sb = sb.tile([P, N // P], F32, name="sp_sb")
+        with nc.allow_non_contiguous_dma(reason="one weight a partition"):
+            nc.sync.dma_start(so_sb[:], so.rearrange("(h p) o -> p (h o)", p=P))
+            nc.sync.dma_start(sp_sb[:], sp.rearrange("(h p) o -> p (h o)", p=P))
+
+        wg_plane = sb.tile([P, R], U8, name="wg_plane", align_bytes=64)
+        nc.vector.tensor_copy(wg_plane[:].rearrange("p (t q) -> p q t", t=PACK),
+                              wt_plane[:].indirect(list_r[:]))
+        wg_listed = sb.tile([P, R], U16, name="wg_listed", align_bytes=64)
+        nc.vector.tensor_copy(wg_listed[:], wt_tab[:].indirect(list_r[:]))
+        xg_words = sb.tile([P, J], U32, name="xg_words", align_bytes=64)
+        nc.vector.tensor_copy(xg_words[:], xt_tab[:].bitcast(U32).indirect(list_j[:]))
+        xg_plane = sb.tile([P, J], U8, name="xg_plane", align_bytes=64)
+        nc.vector.tensor_copy(xg_plane[:], xt_plane[:].indirect(list_j[:]))
+
+        hid = sb.tile([P, PACK * O], BF16, name="hid", align_bytes=64)
+        a_ps = [ps.tile([P, J], F32, name="a_ps%d" % t) for t in range(PACK)]
+        for t in range(PACK):
+            wg_words = sb.tile([P, P], U16, name="wg_words%d" % t, align_bytes=64)
+            nc.vector.tensor_copy(wg_words[:], wg_listed[:, t : R : PACK])
+            nc.tensor.matmul_mx(out=a_ps[t][:], lhsT=wg_words[:].bitcast(E2M1X4),
+                                lhsT_scale=wg_plane[:, t * P : (t + 1) * P],
+                                rhs=xg_words[:].bitcast(E5M2X4), rhs_scale=xg_plane[:], start=True, stop=True)
+        for t in range(PACK):
+            a_sb = sb.tile([P, J], F32, name="a_sb%d" % t)
+            nc.vector.tensor_copy(a_sb[:], a_ps[t][:])
+            nc.scalar.activation(hid[:, t : PACK * O : PACK], a_sb[:].indirect(list_o[:]), COPY,
+                                 scale=sa_sb[:, t : t + 1])
+
+        hid_words = sb.tile([P, O], U32, name="hid_words", align_bytes=64)
+        hid_plane = sb.tile([P, O], U8, name="hid_plane", align_bytes=64)
+        nc.vector.quantize_mx(out=hid_words[:].bitcast(E4M3X4), scales=hid_plane[:], in_=hid[:])
+
+        sides = ((wb_sb, E2M1X4, wb_plane, so_sb, list_a), (wc_sb, E4M3X4, wc_plane, sp_sb, list_b))
+        for h in range(N // P):
+            rows = slice(h * P, (h + 1) * P)
+            for s, (words, fmt, plane, weight, places) in enumerate(sides):
+                acc = ps.tile([P, O], F32, name="acc%d%d" % (s, h))
+                nc.tensor.matmul_mx(out=acc[:], lhsT=words[:, rows].bitcast(fmt), lhsT_scale=plane[:, rows],
+                                    rhs=hid_words[:].bitcast(E4M3X4), rhs_scale=hid_plane[:], start=True, stop=True)
+                outcome = sb.tile([P, O], F32, name="outcome%d%d" % (s, h))
+                nc.vector.tensor_copy(outcome[:], acc[:])
+                nc.scalar.activation(pages[s][h][:].indirect(places[:]), outcome[:], COPY, scale=weight[:, h : h + 1])
+        for h in range(N // P):
+            larger = sb.tile([P, E], F32, name="larger%d" % h)
+            nc.vector.tensor_tensor(larger[:], pages[0][h][:], pages[1][h][:], MAX)
+            nc.sync.dma_start(out[h * P : (h + 1) * P, :], larger[:])

@@ -34,7 +34,7 @@ def tile_list_twooutcomes_kernel(tc, xt_words, xt_scales, wt_words, wt_scales, s
             return tile
 
         def zeroed_plane(width, name):
-            plane = sb.tile([P, width], U8, name=name, align_bytes=64)
+            plane = sb.tile([P, width], U8, name=name, tag=name, align_bytes=64)
             nc.vector.memset(plane[:].bitcast(I32), 0)
             return plane
 
@@ -52,10 +52,10 @@ def tile_list_twooutcomes_kernel(tc, xt_words, xt_scales, wt_words, wt_scales, s
             for s in range(2):
                 nc.vector.memset(pages[s][h][:], 0.0)
 
-        list_r = load_list(offs, "list_r")
-        load_plane(wt_plane, wt_scales)
         wt_tab = sb.tile([P, V], U16, name="wt_tab", align_bytes=64)
         nc.sync.dma_start(wt_tab[:].bitcast(I32), wt_words[0].bitcast(I32))
+        list_r = load_list(offs, "list_r")
+        load_plane(wt_plane, wt_scales)
         list_j = load_list(offs2, "list_j")
         xt_tab = sb.tile([P, T], I32, name="xt_tab", align_bytes=64)
         nc.sync.dma_start(xt_tab[:], xt_words[0].rearrange("p n t -> p (n t)").bitcast(I32))
@@ -63,59 +63,90 @@ def tile_list_twooutcomes_kernel(tc, xt_words, xt_scales, wt_words, wt_scales, s
         list_o = load_list(offs3, "list_o")
         sa_sb = sb.tile([P, PACK], F32, name="sa_sb")
         nc.sync.dma_start(sa_sb[:], sa.rearrange("(p t) o -> p (t o)", t=PACK))
-        wb_sb = sb.tile([P, N], U16, name="wb_sb", align_bytes=64)
-        nc.sync.dma_start(wb_sb[:].bitcast(I32), wb_words[0].bitcast(I32))
         wc_sb = sb.tile([P, N], I32, name="wc_sb", align_bytes=64)
         nc.sync.dma_start(wc_sb[:], wc_words[0].rearrange("p n t -> p (n t)").bitcast(I32))
-        load_plane(wb_plane, wb_scales)
-        load_plane(wc_plane, wc_scales)
-        list_a = load_list(offs4, "list_a")
+        wb_sb = sb.tile([P, N], U16, name="wb_sb", align_bytes=64)
+        nc.sync.dma_start(wb_sb[:].bitcast(I32), wb_words[0].bitcast(I32))
         list_b = load_list(offs5, "list_b")
+        list_a = load_list(offs4, "list_a")
         so_sb = sb.tile([P, N // P], F32, name="so_sb")
         sp_sb = sb.tile([P, N // P], F32, name="sp_sb")
         with nc.allow_non_contiguous_dma(reason="one weight a partition"):
-            nc.sync.dma_start(so_sb[:], so.rearrange("(h p) o -> p (h o)", p=P))
             nc.sync.dma_start(sp_sb[:], sp.rearrange("(h p) o -> p (h o)", p=P))
+            nc.sync.dma_start(so_sb[:], so.rearrange("(h p) o -> p (h o)", p=P))
+        load_plane(wc_plane, wc_scales)
+        load_plane(wb_plane, wb_scales)
 
+        wg_listed = sb.tile([P, R], U16, name="wg_listed", align_bytes=64)
+        nc.vector.tensor_copy(wg_listed[:], wt_tab[:].indirect(list_r[:]))
         wg_plane = sb.tile([P, R], U8, name="wg_plane", align_bytes=64)
         nc.vector.tensor_copy(wg_plane[:].rearrange("p (t q) -> p q t", t=PACK),
                               wt_plane[:].indirect(list_r[:]))
-        wg_listed = sb.tile([P, R], U16, name="wg_listed", align_bytes=64)
-        nc.vector.tensor_copy(wg_listed[:], wt_tab[:].indirect(list_r[:]))
         xg_words = sb.tile([P, J], U32, name="xg_words", align_bytes=64)
         nc.vector.tensor_copy(xg_words[:], xt_tab[:].bitcast(U32).indirect(list_j[:]))
+        wg_first = sb.tile([P, P], U16, name="wg_first", tag="wt_plane", align_bytes=64)
+        nc.vector.tensor_copy(wg_first[:], wg_listed[:, 0:R:PACK])
         xg_plane = sb.tile([P, J], U8, name="xg_plane", align_bytes=64)
         nc.vector.tensor_copy(xg_plane[:], xt_plane[:].indirect(list_j[:]))
 
-        hid = sb.tile([P, PACK * O], BF16, name="hid", align_bytes=64)
-        a_ps = [ps.tile([P, J], F32, name="a_ps%d" % t) for t in range(PACK)]
+        wg_rest = sb.tile([P, (PACK - 1) * P], U16, name="wg_rest", tag="xt_plane", align_bytes=64)
+        for t in range(1, PACK):
+            nc.vector.tensor_copy(wg_rest[:, (t - 1) * P : t * P], wg_listed[:, t:R:PACK])
+        wg_words = [wg_first[:]] + [wg_rest[:, (t - 1) * P : t * P] for t in range(1, PACK)]
+
+        a_sb = []
         for t in range(PACK):
-            wg_words = sb.tile([P, P], U16, name="wg_words%d" % t, align_bytes=64)
-            nc.vector.tensor_copy(wg_words[:], wg_listed[:, t : R : PACK])
-            nc.tensor.matmul_mx(out=a_ps[t][:], lhsT=wg_words[:].bitcast(E2M1X4),
+            a_ps = ps.tile([P, J], F32, name="a_ps%d" % t, tag="bank%d" % t)
+            nc.tensor.matmul_mx(out=a_ps[:], lhsT=wg_words[t].bitcast(E2M1X4),
                                 lhsT_scale=wg_plane[:, t * P : (t + 1) * P],
                                 rhs=xg_words[:].bitcast(E5M2X4), rhs_scale=xg_plane[:], start=True, stop=True)
-        for t in range(PACK):
-            a_sb = sb.tile([P, J], F32, name="a_sb%d" % t)
-            nc.vector.tensor_copy(a_sb[:], a_ps[t][:])
-            nc.scalar.activation(hid[:, t : PACK * O : PACK], a_sb[:].indirect(list_o[:]), COPY,
-                                 scale=sa_sb[:, t : t + 1])
+            a_rows = sb.tile([P, J], F32, name="a_rows%d" % t)
+            if t == 0:
+                nc.scalar.copy(a_rows[:], a_ps[:])
+            else:
+                nc.vector.tensor_copy(a_rows[:], a_ps[:])
+            a_sb.append(a_rows)
 
+        HALF = O // 2
+        q_parts = {}
         hid_words = sb.tile([P, O], U32, name="hid_words", align_bytes=64)
         hid_plane = sb.tile([P, O], U8, name="hid_plane", align_bytes=64)
-        nc.vector.quantize_mx(out=hid_words[:].bitcast(E4M3X4), scales=hid_plane[:], in_=hid[:])
+        for u, order in enumerate((range(PACK), reversed(range(PACK)))):
+            hid = sb.tile([P, PACK * HALF], BF16, name="hid%d" % u, align_bytes=64)
+            part = list_o[:, u * HALF // 16 : (u + 1) * HALF // 16]
+            for t in order:
+                nc.scalar.activation(hid[:, t : PACK * HALF : PACK], a_sb[t][:].indirect(part), COPY,
+                                     scale=sa_sb[:, t : t + 1])
+            cols = slice(u * HALF, (u + 1) * HALF)
+            nc.vector.quantize_mx(out=hid_words[:, cols].bitcast(E4M3X4), scales=hid_plane[:, cols], in_=hid[:])
+            for h in range(N // P):
+                rows = slice(h * P, (h + 1) * P)
+                q_ps = ps.tile([P, HALF], F32, name="q_ps%d%d" % (u, h), tag="bank%d" % (2 * u + h))
+                nc.tensor.matmul_mx(out=q_ps[:], lhsT=wc_sb[:, rows].bitcast(E4M3X4), lhsT_scale=wc_plane[:, rows],
+                                    rhs=hid_words[:, cols].bitcast(E4M3X4), rhs_scale=hid_plane[:, cols],
+                                    start=True, stop=True)
+                q_sb = sb.tile([P, HALF], F32, name="q_sb%d%d" % (u, h))
+                nc.vector.tensor_copy(q_sb[:], q_ps[:])
+                q_parts[u, h] = q_sb
 
-        sides = ((wb_sb, E2M1X4, wb_plane, so_sb, list_a), (wc_sb, E4M3X4, wc_plane, sp_sb, list_b))
+        for u in range(2):
+            part = list_b[:, u * HALF // 16 : (u + 1) * HALF // 16]
+            for h in range(N // P):
+                nc.scalar.activation(pages[1][h][:].indirect(part), q_parts[u, h][:], COPY,
+                                     scale=sp_sb[:, h : h + 1])
+
         for h in range(N // P):
             rows = slice(h * P, (h + 1) * P)
-            for s, (words, fmt, plane, weight, places) in enumerate(sides):
-                acc = ps.tile([P, O], F32, name="acc%d%d" % (s, h))
-                nc.tensor.matmul_mx(out=acc[:], lhsT=words[:, rows].bitcast(fmt), lhsT_scale=plane[:, rows],
-                                    rhs=hid_words[:].bitcast(E4M3X4), rhs_scale=hid_plane[:], start=True, stop=True)
-                outcome = sb.tile([P, O], F32, name="outcome%d%d" % (s, h))
-                nc.vector.tensor_copy(outcome[:], acc[:])
-                nc.scalar.activation(pages[s][h][:].indirect(places[:]), outcome[:], COPY, scale=weight[:, h : h + 1])
-        for h in range(N // P):
-            larger = sb.tile([P, E], F32, name="larger%d" % h)
-            nc.vector.tensor_tensor(larger[:], pages[0][h][:], pages[1][h][:], MAX)
-            nc.sync.dma_start(out[h * P : (h + 1) * P, :], larger[:])
+            p_ps = ps.tile([P, O], F32, name="p_ps%d" % h)
+            nc.tensor.matmul_mx(out=p_ps[:], lhsT=wb_sb[:, rows].bitcast(E2M1X4), lhsT_scale=wb_plane[:, rows],
+                                rhs=hid_words[:].bitcast(E4M3X4), rhs_scale=hid_plane[:], start=True, stop=True)
+            p_sb = sb.tile([P, O], F32, name="p_sb%d" % h)
+            nc.vector.tensor_copy(p_sb[:], p_ps[:])
+            nc.scalar.activation(pages[0][h][:].indirect(list_a[:]), p_sb[:], COPY, scale=so_sb[:, h : h + 1])
+            pieces = (nc.sync,) if h == 0 else (nc.sync, nc.scalar)
+            width = E // len(pieces)
+            for c, queue in enumerate(pieces):
+                cols = slice(c * width, (c + 1) * width)
+                larger = sb.tile([P, width], F32, name="larger%d%d" % (h, c))
+                nc.vector.tensor_tensor(larger[:], pages[0][h][:, cols], pages[1][h][:, cols], MAX)
+                queue.dma_start(out[rows, cols], larger[:])

@@ -143,10 +143,6 @@ def tile_list_twooutcomes_kernel(tc, xt_words, xt_scales, wt_words, wt_scales, s
             p_sb = sb.tile([P, O], F32, name="p_sb%d" % h)
             nc.vector.tensor_copy(p_sb[:], p_ps[:])
             nc.scalar.activation(pages[0][h][:].indirect(list_a[:]), p_sb[:], COPY, scale=so_sb[:, h : h + 1])
-            pieces = (nc.sync,) if h == 0 else (nc.sync, nc.scalar)
-            width = E // len(pieces)
-            for c, queue in enumerate(pieces):
-                cols = slice(c * width, (c + 1) * width)
-                larger = sb.tile([P, width], F32, name="larger%d%d" % (h, c))
-                nc.vector.tensor_tensor(larger[:], pages[0][h][:, cols], pages[1][h][:, cols], MAX)
-                queue.dma_start(out[rows, cols], larger[:])
+            larger = sb.tile([P, E], F32, name="larger%d" % h)
+            nc.vector.tensor_tensor(larger[:], pages[0][h][:], pages[1][h][:], MAX)
+            nc.sync.dma_start(out[rows, :], larger[:])

from contextlib import ExitStack

import concourse.mybir as mybir

F32 = mybir.dt.float32
BF16 = mybir.dt.bfloat16
I32 = mybir.dt.int32
U32 = mybir.dt.uint32
U16 = mybir.dt.uint16
U8 = mybir.dt.uint8
E4M3X4 = mybir.dt.float8_e4m3fn_x4
E5M2X4 = mybir.dt.float8_e5m2_x4
E2M1X4 = mybir.dt.float4_e2m1fn_x4
COPY = mybir.ActivationFunctionType.Copy
MAX = mybir.AluOpType.max

K, T, J, R, V, O, N, E = 512, 1024, 256, 512, 1024, 128, 256, 256
P = 128
PACK = 4
QUADS = 4
FLOPS = 2 * K * R * J + 2 * 2 * R * N * O


def tile_list_twooutcomes_kernel(tc, xt_words, xt_scales, wt_words, wt_scales, sa, wb_words, wb_scales,
                                     wc_words, wc_scales, so, sp, offs, offs2, offs3, offs4, offs5, out):
    nc = tc.nc
    with ExitStack() as ctx:
        sb = ctx.enter_context(tc.tile_pool(name="sb", bufs=1))
        ps = ctx.enter_context(tc.psum_pool(name="ps", bufs=1))

        def load_list(src, name):
            tile = sb.tile(list(src.shape), U16, name=name)
            nc.sync.dma_start(tile[:], src)
            return tile

        def zeroed_plane(width, name):
            plane = sb.tile([P, width], U8, name=name, tag=name, align_bytes=64)
            nc.vector.memset(plane[:].bitcast(I32), 0)
            return plane

        def load_plane(plane, scales):
            for q in range(QUADS):
                nc.sync.dma_start(plane[32 * q : 32 * q + 4, :].bitcast(I32),
                                  scales[0, 4 * q : 4 * q + 4, :].bitcast(I32))

        wt_plane = zeroed_plane(V, "wt_plane")
        xt_plane = zeroed_plane(T, "xt_plane")
        wb_plane = zeroed_plane(N, "wb_plane")
        wc_plane = zeroed_plane(N, "wc_plane")
        pages = [[sb.tile([P, E], F32, name="page%d%d" % (s, h)) for h in range(N // P)] for s in range(2)]
        for h in range(N // P):
            for s in range(2):
                nc.vector.memset(pages[s][h][:], 0.0)

        wt_tab = sb.tile([P, V], U16, name="wt_tab", align_bytes=64)
        nc.sync.dma_start(wt_tab[:].bitcast(I32), wt_words[0].bitcast(I32))
        list_r = load_list(offs, "list_r")
        load_plane(wt_plane, wt_scales)
        list_j = load_list(offs2, "list_j")
        xt_tab = sb.tile([P, T], I32, name="xt_tab", align_bytes=64)
        nc.sync.dma_start(xt_tab[:], xt_words[0].rearrange("p n t -> p (n t)").bitcast(I32))
        load_plane(xt_plane, xt_scales)
        list_o = load_list(offs3, "list_o")
        sa_sb = sb.tile([P, PACK], F32, name="sa_sb")
        nc.sync.dma_start(sa_sb[:], sa.rearrange("(p t) o -> p (t o)", t=PACK))
        wc_sb = sb.tile([P, N], I32, name="wc_sb", align_bytes=64)
        nc.sync.dma_start(wc_sb[:], wc_words[0].rearrange("p n t -> p (n t)").bitcast(I32))
        wb_sb = sb.tile([P, N], U16, name="wb_sb", align_bytes=64)
        nc.sync.dma_start(wb_sb[:].bitcast(I32), wb_words[0].bitcast(I32))
        list_b = load_list(offs5, "list_b")
        list_a = load_list(offs4, "list_a")
        so_sb = sb.tile([P, N // P], F32, name="so_sb")
        sp_sb = sb.tile([P, N // P], F32, name="sp_sb")
        with nc.allow_non_contiguous_dma(reason="one weight a partition"):
            nc.sync.dma_start(sp_sb[:], sp.rearrange("(h p) o -> p (h o)", p=P))
            nc.sync.dma_start(so_sb[:], so.rearrange("(h p) o -> p (h o)", p=P))
        load_plane(wc_plane, wc_scales)
        load_plane(wb_plane, wb_scales)

        wg_listed = sb.tile([P, R], U16, name="wg_listed", align_bytes=64)
        nc.vector.tensor_copy(wg_listed[:], wt_tab[:].indirect(list_r[:]))
        wg_plane = sb.tile([P, R], U8, name="wg_plane", align_bytes=64)
        nc.vector.tensor_copy(wg_plane[:].rearrange("p (t q) -> p q t", t=PACK),
                              wt_plane[:].indirect(list_r[:]))
        xg_words = sb.tile([P, J], U32, name="xg_words", align_bytes=64)
        nc.vector.tensor_copy(xg_words[:], xt_tab[:].bitcast(U32).indirect(list_j[:]))
        wg_first = sb.tile([P, P], U16, name="wg_first", tag="wt_plane", align_bytes=64)
        nc.vector.tensor_copy(wg_first[:], wg_listed[:, 0:R:PACK])
        xg_plane = sb.tile([P, J], U8, name="xg_plane", align_bytes=64)
        nc.vector.tensor_copy(xg_plane[:], xt_plane[:].indirect(list_j[:]))

        wg_rest = sb.tile([P, (PACK - 1) * P], U16, name="wg_rest", tag="xt_plane", align_bytes=64)
        for t in range(1, PACK):
            nc.vector.tensor_copy(wg_rest[:, (t - 1) * P : t * P], wg_listed[:, t:R:PACK])
        wg_words = [wg_first[:]] + [wg_rest[:, (t - 1) * P : t * P] for t in range(1, PACK)]

        a_sb = []
        for t in range(PACK):
            a_ps = ps.tile([P, J], F32, name="a_ps%d" % t, tag="bank%d" % t)
            nc.tensor.matmul_mx(out=a_ps[:], lhsT=wg_words[t].bitcast(E2M1X4),
                                lhsT_scale=wg_plane[:, t * P : (t + 1) * P],
                                rhs=xg_words[:].bitcast(E5M2X4), rhs_scale=xg_plane[:], start=True, stop=True)
            a_rows = sb.tile([P, J], F32, name="a_rows%d" % t)
            if t == 0:
                nc.scalar.copy(a_rows[:], a_ps[:])
            else:
                nc.vector.tensor_copy(a_rows[:], a_ps[:])
            a_sb.append(a_rows)

        HALF = O // 2
        q_parts = {}
        hid_words = sb.tile([P, O], U32, name="hid_words", align_bytes=64)
        hid_plane = sb.tile([P, O], U8, name="hid_plane", align_bytes=64)
        for u, order in enumerate((range(PACK), reversed(range(PACK)))):
            hid = sb.tile([P, PACK * HALF], BF16, name="hid%d" % u, align_bytes=64)
            part = list_o[:, u * HALF // 16 : (u + 1) * HALF // 16]
            for t in order:
                nc.scalar.activation(hid[:, t : PACK * HALF : PACK], a_sb[t][:].indirect(part), COPY,
                                     scale=sa_sb[:, t : t + 1])
            cols = slice(u * HALF, (u + 1) * HALF)
            nc.vector.quantize_mx(out=hid_words[:, cols].bitcast(E4M3X4), scales=hid_plane[:, cols], in_=hid[:])
            for h in range(N // P):
                rows = slice(h * P, (h + 1) * P)
                q_ps = ps.tile([P, HALF], F32, name="q_ps%d%d" % (u, h), tag="bank%d" % (2 * u + h))
                nc.tensor.matmul_mx(out=q_ps[:], lhsT=wc_sb[:, rows].bitcast(E4M3X4), lhsT_scale=wc_plane[:, rows],
                                    rhs=hid_words[:, cols].bitcast(E4M3X4), rhs_scale=hid_plane[:, cols],
                                    start=True, stop=True)
                q_sb = sb.tile([P, HALF], F32, name="q_sb%d%d" % (u, h))
                nc.vector.tensor_copy(q_sb[:], q_ps[:])
                q_parts[u, h] = q_sb

        for u in range(2):
            part = list_b[:, u * HALF // 16 : (u + 1) * HALF // 16]
            for h in range(N // P):
                nc.scalar.activation(pages[1][h][:].indirect(part), q_parts[u, h][:], COPY,
                                     scale=sp_sb[:, h : h + 1])

        for h in range(N // P):
            rows = slice(h * P, (h + 1) * P)
            p_ps = ps.tile([P, O], F32, name="p_ps%d" % h)
            nc.tensor.matmul_mx(out=p_ps[:], lhsT=wb_sb[:, rows].bitcast(E2M1X4), lhsT_scale=wb_plane[:, rows],
                                rhs=hid_words[:].bitcast(E4M3X4), rhs_scale=hid_plane[:], start=True, stop=True)
            p_sb = sb.tile([P, O], F32, name="p_sb%d" % h)
            nc.vector.tensor_copy(p_sb[:], p_ps[:])
            nc.scalar.activation(pages[0][h][:].indirect(list_a[:]), p_sb[:], COPY, scale=so_sb[:, h : h + 1])
            larger = sb.tile([P, E], F32, name="larger%d" % h)
            nc.vector.tensor_tensor(larger[:], pages[0][h][:], pages[1][h][:], MAX)
            nc.sync.dma_start(out[rows, :], larger[:])
